import numpy as np, ml_dtypes
CORES = [24,26,29,31,48,50,53,55]
N = 8
import mx_ref
NC, G = 256, 2
C = np.float32(0.00672)
BF = ml_dtypes.bfloat16
def cut(t, i, w=512):
    return t[:, w * i:w * i + w]
def tile(rs):
    return np.stack(rs, axis=2).reshape(128, -1).astype(BF)
def layer(w, X):
    out = []
    for i in range(G):
        for t in range(len(X)):
            p = mx_ref.matmul(mx_ref.quantize(cut(w, len(X) * i + t)), X[t])
            z = p if t == 0 else z + p
        out.append(z)
    return out
def act(Z):
    return [np.maximum(s * z, 0) * C for z in Z for s in (1, -1)]
def setup_inputs(rng):
    def f(*shape):
        return mx_ref.flush((rng.standard_normal(shape, dtype=np.float32) * np.exp2(rng.integers(-2, 3, shape[:-1] + (1,)))).astype(BF))
    return {"x": f(N, 128, 4 * NC), "w1": f(N, 128, G * N * 512), "w2": f(N, 128, 512)}
def setup_inputs_blocks(rng):
    d = setup_inputs(rng)
    for k in ("x", "w1", "w2"): d[k] = mx_ref.spread(d[k], rng, 4)
    return d
def setup_inputs_wide(rng):
    d = setup_inputs(rng)
    for k in ("x", "w1", "w2"): d[k] = mx_ref.flush((d[k].astype(np.float32) * np.exp2(rng.integers(-6, 7, (N, 1, 1))).astype(np.float32)).astype(BF))
    return d
def reference(x, w1, w2, own=None):
    X = [mx_ref.quantize(x[j]) for j in range(N)]
    h = np.stack([tile(act(layer(w1[r], X))) for r in range(N)])
    use = h if own is None else own["h"]
    H = [mx_ref.quantize(use[j]) for j in range(N)]
    y = np.zeros((N, 128, N * NC), np.float32)
    for r in range(N):
        qw = mx_ref.quantize(w2[r])
        for j in range(N):
            y[r][:, NC * j:NC * j + NC] = mx_ref.matmul(qw, H[j])
    return {"h": h, "y": y}

@@ -1,0 +1,262 @@
+import numpy as np
+from concourse.bass import DstId, RemoteDMATransfer
+from concourse.mybir import dt, AluOpType, ActivationFunctionType
+
+N = 8
+NSIM = 64
+NC = 256
+WC = 128
+CACT = float(np.float32(0.00672))
+
+SCRATCH = {
+    "xb": ("sbuf", [128, 4 * NC], "bfloat16"),
+    "w1b": ("sbuf", [128, 2 * N * 4 * WC], "bfloat16"),
+    "w2b": ("sbuf", [128, 4 * WC], "bfloat16"),
+    "hb": ("sbuf", [128, 4 * NC], "bfloat16"),
+    "yb": ("sbuf", [128, N * NC], "float32"),
+    "xq": ("sbuf", [128, N * NC], "float8_e4m3fn_x4"),
+    "xs": ("sbuf", [128, N * NC], "uint8"),
+    "hq": ("sbuf", [128, N * NC], "float8_e4m3fn_x4"),
+    "hs": ("sbuf", [128, N * NC], "uint8"),
+    "w1q": ("sbuf", [128, 2 * N * WC], "float8_e4m3fn_x4"),
+    "w1s": ("sbuf", [128, 2 * N * WC], "uint8"),
+    "w2q": ("sbuf", [128, WC], "float8_e4m3fn_x4"),
+    "w2s": ("sbuf", [128, WC], "uint8"),
+    "ps": ("psum", [128, 8 * 512], "float32"),
+}
+SEMAPHORES = (
+    ["%s%s%d" % (ph, k, j) for ph in "xh" for k in "pc" for j in range(N)]
+    + ["lx", "la", "lb", "lc", "ld", "l2"]
+    + ["qx", "qa", "qb", "qc", "q2", "qh"] + ["qd%d" % n for n in range(4)]
+    + ["z0", "z1", "act"]
+    + ["y%d" % n for n in range(N)] + ["c%d" % n for n in range(N)]
+    + ["gx", "gh", "snt", "sts", "stc"]
+)
+
+
+def _bits(m):
+    return bin(m).count("1")
+
+
+def _plan(T, topo):
+    cores = list(T.cores)
+    routes = []
+    for r in cores:
+        near = [c for c in cores if topo.chip(c) == topo.chip(r) and c != r]
+        far = [c for c in cores if topo.chip(c) != topo.chip(r)]
+        near.sort(key=lambda c: topo.die(c) != topo.die(r))
+
+        def spare(ch, die):
+            return [c for c in range(NSIM) if topo.chip(c) == ch and topo.die(c) == die and c not in cores]
+
+        if topo.may_write(r, far[0]):
+            carrier = r
+        else:
+            carrier = [c for c in spare(topo.chip(r), topo.die(r)) if topo.may_write(c, far[0])][0]
+        spreader = [c for c in spare(topo.chip(far[0]), topo.die(carrier))
+                    if topo.may_write(c, r) == (carrier != r)][0]
+        on = topo.mask(r, near[0])
+        if carrier == r:
+            off = topo.mask(r, spreader)
+            rest = on & ~off
+            first = [(off, [spreader]), (rest, [near[0]])]
+            second = [(off, [near[1]]), (rest, [near[2]])]
+            hops = []
+        else:
+            first = [(on, [carrier])]
+            second = [(on, near)]
+            hops = [(carrier, [(topo.mask(carrier, spreader), [spreader])])]
+        hops.append((spreader, [(topo.mask(spreader, far[0]), far)]))
+        cnt = {}
+        for parts in [first, second] + [h[1] for h in hops]:
+            for m, ds in parts:
+                for d in ds:
+                    cnt[d] = _bits(m)
+        routes.append({"first": first, "second": second, "hops": hops, "cnt": cnt, "late": carrier != r})
+    return routes
+
+
+def _send(g, topo, parts, buf, j, codes, remote_sem, local_sem):
+    def view():
+        v = buf[:, NC * j:NC * j + NC]
+        return v.bitcast(dt.uint8) if codes else v
+
+    if len(parts) == 1 and len(parts[0][1]) == 1:
+        m, ds = parts[0]
+        rid, pid, _se = topo.addr(ds[0])
+        g.remote_dma(out_ap=view(), in_ap=view(), remote_sem=remote_sem, local_sem=local_sem, pid=pid,
+                     routing_id=rid, dma_engine_mask=m)
+        return _bits(m)
+    trs = []
+    for m, ds in parts:
+        ids = [DstId(rid=topo.addr(d)[0], pnc=topo.addr(d)[1]) for d in ds]
+        trs.append(RemoteDMATransfer(dst_ids=ids, dma_engine_mask=m, remote_sem=remote_sem,
+                                     srcs=[view()], dsts=[view() for d in ds]))
+    g.remote_dma_fused(trs, local_sem=local_sem)
+    return sum(_bits(m) for m, ds in parts)
+
+
+def _bufs(T, ph):
+    return (T.xq, T.xs) if ph == "x" else (T.hq, T.hs)
+
+
+def _spare_program(g, core, T, topo, routes):
+    jobs = []
+    for depth in (0, 1):
+        for j, rt in enumerate(routes):
+            hops = rt["hops"]
+            for n, (who, parts) in enumerate(hops):
+                if who == core and (n == len(hops) - 1) == (depth == 1):
+                    jobs.append((j, parts, rt["cnt"][core]))
+    if not jobs:
+        return
+    left = 0
+    for ph in "xh":
+        q, s = _bufs(T, ph)
+        for j, parts, cnt in jobs:
+            g.wait_ge(T.sem["%sp%d" % (ph, j)], cnt)
+            left += _send(g, topo, parts, s, j, False, T.sem["%sp%d" % (ph, j)], T.sem.snt)
+            g.wait_ge(T.sem["%sc%d" % (ph, j)], cnt)
+            left += _send(g, topo, parts, q, j, True, T.sem["%sc%d" % (ph, j)], T.sem.snt)
+    g.wait_ge(T.sem.snt, left)
+
+
+def rank_program(g, core, T, topo):
+    routes = _plan(T, topo)
+    me = T.rank_of(core)
+    if me is None:
+        _spare_program(g, core, T, topo, routes)
+        return
+    S = T.sem
+    cores = list(T.cores)
+    mine = [j for j in range(N) if topo.chip(cores[j]) == topo.chip(core)]
+    far = [j for j in range(N) if j not in mine]
+    near = sorted([j for j in mine if j != me], key=lambda j: (topo.die(cores[j]) != topo.die(core), routes[j]["late"]))
+    far = sorted(far, key=lambda j: (routes[j]["late"], topo.die(cores[j]) != topo.die(core)))
+    rt = routes[me]
+
+    def w1cols(i, js, w):
+        return slice(w * (N * i + min(js)), w * (N * i + max(js) + 1))
+
+    def own(w=NC):
+        return slice(w * me, w * me + w)
+
+    gate = sum(_bits(m) for m, ds in rt["second"])
+    g.sync.dma_start(T.xb[:], T.x[:]).then_inc(S.lx, 16)
+    c = w1cols(0, mine, 4 * WC)
+    g.sync.dma_start(T.w1b[:, c], T.w1[:, c]).then_inc(S.la, 16)
+    g.sync.wait_ge(S.gx, gate)
+    g.scalar.wait_ge(S.gx, gate)
+    c = w1cols(1, mine, 4 * WC)
+    g.sync.dma_start(T.w1b[:, c], T.w1[:, c]).then_inc(S.lb, 16)
+    g.scalar.dma_start(T.w2b[:], T.w2[:]).then_inc(S.l2, 16)
+    c = w1cols(0, far, 4 * WC)
+    g.sync.dma_start(T.w1b[:, c], T.w1[:, c]).then_inc(S.lc, 16)
+    c = w1cols(1, far, 4 * WC)
+    g.scalar.dma_start(T.w1b[:, c], T.w1[:, c]).then_inc(S.ld, 16)
+
+    left = 0
+    for ph, ready, gsem in (("x", S.qx, S.gx), ("h", S.qh, S.gh)):
+        q, s = _bufs(T, ph)
+        sp, sc = S["%sp%d" % (ph, me)], S["%sc%d" % (ph, me)]
+        g.wait_ge(ready, 1)
+        left += _send(g, topo, rt["first"], s, me, False, sp, S.snt)
+        left += _send(g, topo, rt["first"], q, me, True, sc, S.snt)
+        _send(g, topo, rt["second"], s, me, False, sp, gsem)
+        left += _send(g, topo, rt["second"], q, me, True, sc, S.snt)
+    g.wait_ge(S.snt, left)
+
+    v = g.vector
+    v.wait_ge(S.lx, 16)
+    v.quantize_mx(T.xq[:, own()], T.xs[:, own()], T.xb[:]).then_inc(S.qx, 1)
+    for i, js, ld, qs in ((0, mine, S.la, S.qa), (1, mine, S.lb, S.qb)):
+        v.wait_ge(ld, 16)
+        c = w1cols(i, js, WC)
+        v.quantize_mx(T.w1q[:, c], T.w1s[:, c], T.w1b[:, w1cols(i, js, 4 * WC)]).then_inc(qs, 1)
+    v.wait_ge(S.l2, 16)
+    v.quantize_mx(T.w2q[:], T.w2s[:], T.w2b[:]).then_inc(S.q2, 1)
+    v.wait_ge(S.lc, 16)
+    c = w1cols(0, far, WC)
+    v.quantize_mx(T.w1q[:, c], T.w1s[:, c], T.w1b[:, w1cols(0, far, 4 * WC)]).then_inc(S.qc, 1)
+    v.wait_ge(S.ld, 16)
+    for n, j in enumerate(far):
+        c = w1cols(1, [j], WC)
+        v.quantize_mx(T.w1q[:, c], T.w1s[:, c], T.w1b[:, w1cols(1, [j], 4 * WC)]).then_inc(S["qd%d" % n], 1)
+
+    t = g.tensor
+
+    def landed(ph, j):
+        if j == me:
+            t.wait_ge(S.qx if ph == "x" else S.qh, 1)
+        else:
+            t.wait_ge(S["%sp%d" % (ph, j)], routes[j]["cnt"][core])
+            t.wait_ge(S["%sc%d" % (ph, j)], routes[j]["cnt"][core])
+
+    def mm1(i, j, start, stop):
+        cw = w1cols(i, [j], WC)
+        cx = slice(NC * j, NC * j + NC)
+        return t.matmul_mx(T.ps[:, 512 * i:512 * i + NC], T.w1q[:, cw], T.w1s[:, cw], T.xq[:, cx], T.xs[:, cx],
+                           start, stop)
+
+    t.wait_ge(S.qa, 1)
+    for n, j in enumerate([me] + near):
+        landed("x", j)
+        mm1(0, j, n == 0, False)
+        if n == 0:
+            t.wait_ge(S.qb, 1)
+        mm1(1, j, n == 0, False)
+    t.wait_ge(S.qc, 1)
+    early, late = far[:2], far[2:]
+    for j in early:
+        landed("x", j)
+        mm1(0, j, False, False)
+    for n, j in enumerate(early):
+        t.wait_ge(S["qd%d" % n], 1)
+        mm1(1, j, False, False)
+    for n, j in enumerate(late):
+        landed("x", j)
+        ins = mm1(0, j, False, n == 1)
+        if n == 1:
+            ins.then_inc(S.z0, 1)
+    for n, j in enumerate(late):
+        t.wait_ge(S["qd%d" % (2 + n)], 1)
+        ins = mm1(1, j, False, n == 1)
+        if n == 1:
+            ins.then_inc(S.z1, 1)
+
+    W = 4 * NC
+    v.wait_ge(S.z0, 1)
+    v.tensor_scalar(T.hb[:, 0:W:4], T.ps[:, 0:NC], CACT, 0.0, AluOpType.mult, AluOpType.max).then_inc(S.act, 1)
+    v.tensor_scalar(T.hb[:, 1:W:4], T.ps[:, 0:NC], -CACT, 0.0, AluOpType.mult, AluOpType.max).then_inc(S.act, 1)
+    a = g.scalar
+    a.wait_ge(S.z1, 1)
+    a.activation(T.hb[:, 2:W:4], T.ps[:, 512:512 + NC], ActivationFunctionType.Relu, scale=CACT).then_inc(S.act, 1)
+    a.activation(T.hb[:, 3:W:4], T.ps[:, 512:512 + NC], ActivationFunctionType.Relu, scale=-CACT).then_inc(S.act, 1)
+    v.wait_ge(S.act, 4)
+    v.quantize_mx(T.hq[:, own()], T.hs[:, own()], T.hb[:]).then_inc(S.qh, 1)
+
+    g.sync.wait_ge(S.gh, gate)
+    g.sync.wait_ge(S.act, 4)
+    g.sync.dma_start(T.h[:], T.hb[:]).then_inc(S.sts, 16)
+    nsts, nstc = 16, 0
+    t.wait_ge(S.q2, 1)
+    for n, j in enumerate([me] + near + far):
+        b = 512 * ((n + 2) % 8)
+        cy = slice(NC * j, NC * j + NC)
+        landed("h", j)
+        t.matmul_mx(T.ps[:, b:b + NC], T.w2q[:], T.w2s[:], T.hq[:, cy], T.hs[:, cy], True, True).then_inc(
+            S["y%d" % n], 1)
+        if n % 2 == 0:
+            v.wait_ge(S["y%d" % n], 1)
+            v.tensor_copy(T.yb[:, cy], T.ps[:, b:b + NC]).then_inc(S["c%d" % n], 1)
+            g.sync.wait_ge(S["c%d" % n], 1)
+            g.sync.dma_start(T.y[:, cy], T.yb[:, cy]).then_inc(S.sts, 16)
+            nsts += 16
+        else:
+            a.wait_ge(S["y%d" % n], 1)
+            a.activation(T.yb[:, cy], T.ps[:, b:b + NC], ActivationFunctionType.Copy).then_inc(S["c%d" % n], 1)
+            a.wait_ge(S["c%d" % n], 1)
+            a.dma_start(T.y[:, cy], T.yb[:, cy]).then_inc(S.stc, 16)
+            nstc += 16
+    g.sync.wait_ge(S.sts, nsts)
+    a.wait_ge(S.stc, nstc)

@@ -5,6 +5,7 @@ from concourse.mybir import dt, AluOpType, ActivationFunctionType
 N = 8
 NSIM = 64
 NC = 256
+HC = NC // 2
 WC = 128
 CACT = float(np.float32(0.00672))
 
@@ -25,13 +26,14 @@ SCRATCH = {
     "ps": ("psum", [128, 8 * 512], "float32"),
 }
 SEMAPHORES = (
-    ["%s%s%d" % (ph, k, j) for ph in "xh" for k in "pc" for j in range(N)]
-    + ["lx", "la", "lb", "lc", "ld", "l2"]
-    + ["qx", "qa", "qb", "qc", "q2", "qh"] + ["qd%d" % n for n in range(4)]
-    + ["z0", "z1", "act"]
-    + ["y%d" % n for n in range(N)] + ["c%d" % n for n in range(N)]
+    ["%s%s%d" % (ph, k, j) for ph in "xh" for k in "pab" for j in range(N)]
+    + ["lx0", "lx1", "la", "lb", "lc", "ld0", "ld1", "l2"]
+    + ["qx0", "qx1", "qh0", "qh1", "qa", "qb", "qc", "q2"] + ["qd%d" % j for j in range(N)]
+    + ["z%d%d" % (i, a) for i in range(2) for a in range(2)] + ["act0", "act1"]
+    + ["y%d" % n for n in range(2 * N)] + ["c%d" % n for n in range(2 * N)]
     + ["gx", "gh", "snt", "sts", "stc"]
 )
+LONG = ("a", "p", "b")
 
 
 def _bits(m):
@@ -72,14 +74,20 @@ def _plan(T, topo):
             for m, ds in parts:
                 for d in ds:
                     cnt[d] = _bits(m)
-        routes.append({"first": first, "second": second, "hops": hops, "cnt": cnt, "late": carrier != r})
+        whole = [d for m, ds in second for d in ds]
+        routes.append({"first": first, "second": second, "hops": hops, "cnt": cnt, "late": carrier != r,
+                       "whole": whole})
     return routes
 
 
-def _send(g, topo, parts, buf, j, codes, remote_sem, local_sem):
+def _send(g, T, topo, parts, ph, j, kind, local_sem):
+    q, s = (T.xq, T.xs) if ph == "x" else (T.hq, T.hs)
+    lo = NC * j + (HC if kind == "b" else 0)
+    hi = NC * j + (HC if kind == "a" else NC)
+    remote_sem = T.sem["%s%s%d" % (ph, "b" if kind == "w" else kind, j)]
+
     def view():
-        v = buf[:, NC * j:NC * j + NC]
-        return v.bitcast(dt.uint8) if codes else v
+        return s[:, lo:hi] if kind == "p" else q[:, lo:hi].bitcast(dt.uint8)
 
     if len(parts) == 1 and len(parts[0][1]) == 1:
         m, ds = parts[0]
@@ -96,10 +104,6 @@ def _send(g, topo, parts, buf, j, codes, remote_sem, local_sem):
     return sum(_bits(m) for m, ds in parts)
 
 
-def _bufs(T, ph):
-    return (T.xq, T.xs) if ph == "x" else (T.hq, T.hs)
-
-
 def _spare_program(g, core, T, topo, routes):
     jobs = []
     for depth in (0, 1):
@@ -112,12 +116,10 @@ def _spare_program(g, core, T, topo, routes):
         return
     left = 0
     for ph in "xh":
-        q, s = _bufs(T, ph)
         for j, parts, cnt in jobs:
-            g.wait_ge(T.sem["%sp%d" % (ph, j)], cnt)
-            left += _send(g, topo, parts, s, j, False, T.sem["%sp%d" % (ph, j)], T.sem.snt)
-            g.wait_ge(T.sem["%sc%d" % (ph, j)], cnt)
-            left += _send(g, topo, parts, q, j, True, T.sem["%sc%d" % (ph, j)], T.sem.snt)
+            for kind in LONG:
+                g.wait_ge(T.sem["%s%s%d" % (ph, kind, j)], cnt)
+                left += _send(g, T, topo, parts, ph, j, kind, T.sem.snt)
     g.wait_ge(T.sem.snt, left)
 
 
@@ -132,131 +134,141 @@ def rank_program(g, core, T, topo):
     mine = [j for j in range(N) if topo.chip(cores[j]) == topo.chip(core)]
     far = [j for j in range(N) if j not in mine]
     near = sorted([j for j in mine if j != me], key=lambda j: (topo.die(cores[j]) != topo.die(core), routes[j]["late"]))
-    far = sorted(far, key=lambda j: (routes[j]["late"], topo.die(cores[j]) != topo.die(core)))
+    pairs = [sorted(far)[:2], sorted(far)[2:]]
+    early = [j for j in sorted(far) if not routes[j]["late"]]
+    late = [j for j in sorted(far) if routes[j]["late"]]
     rt = routes[me]
 
     def w1cols(i, js, w):
         return slice(w * (N * i + min(js)), w * (N * i + max(js) + 1))
 
-    def own(w=NC):
-        return slice(w * me, w * me + w)
+    def half(j, a, w=1):
+        return slice(w * (NC * j + HC * a), w * (NC * j + HC * a + HC))
 
-    gate = sum(_bits(m) for m, ds in rt["second"])
-    g.sync.dma_start(T.xb[:], T.x[:]).then_inc(S.lx, 16)
+    gate = sum(_bits(m) for m, ds in rt["first"])
+    g.sync.dma_start(T.xb[:, half(0, 0, 4)], T.x[:, half(0, 0, 4)]).then_inc(S.lx0, 16)
+    g.scalar.dma_start(T.xb[:, half(0, 1, 4)], T.x[:, half(0, 1, 4)]).then_inc(S.lx1, 16)
     c = w1cols(0, mine, 4 * WC)
     g.sync.dma_start(T.w1b[:, c], T.w1[:, c]).then_inc(S.la, 16)
     g.sync.wait_ge(S.gx, gate)
-    g.scalar.wait_ge(S.gx, gate)
-    c = w1cols(1, mine, 4 * WC)
-    g.sync.dma_start(T.w1b[:, c], T.w1[:, c]).then_inc(S.lb, 16)
-    g.scalar.dma_start(T.w2b[:], T.w2[:]).then_inc(S.l2, 16)
-    c = w1cols(0, far, 4 * WC)
-    g.sync.dma_start(T.w1b[:, c], T.w1[:, c]).then_inc(S.lc, 16)
-    c = w1cols(1, far, 4 * WC)
-    g.scalar.dma_start(T.w1b[:, c], T.w1[:, c]).then_inc(S.ld, 16)
+    for i, js, ld in ((1, mine, S.lb), (0, far, S.lc), (1, pairs[0], S.ld0), (1, pairs[1], S.ld1)):
+        c = w1cols(i, js, 4 * WC)
+        g.sync.dma_start(T.w1b[:, c], T.w1[:, c]).then_inc(ld, 16)
+    g.sync.dma_start(T.w2b[:], T.w2[:]).then_inc(S.l2, 16)
 
     left = 0
-    for ph, ready, gsem in (("x", S.qx, S.gx), ("h", S.qh, S.gh)):
-        q, s = _bufs(T, ph)
-        sp, sc = S["%sp%d" % (ph, me)], S["%sc%d" % (ph, me)]
-        g.wait_ge(ready, 1)
-        left += _send(g, topo, rt["first"], s, me, False, sp, S.snt)
-        left += _send(g, topo, rt["first"], q, me, True, sc, S.snt)
-        _send(g, topo, rt["second"], s, me, False, sp, gsem)
-        left += _send(g, topo, rt["second"], q, me, True, sc, S.snt)
+    for ph, gsem in (("x", S.gx), ("h", S.gh)):
+        g.wait_ge(S["q%s0" % ph], 1)
+        _send(g, T, topo, rt["first"], ph, me, "a", gsem)
+        g.wait_ge(S["q%s1" % ph], 1)
+        left += _send(g, T, topo, rt["first"], ph, me, "p", S.snt)
+        left += _send(g, T, topo, rt["first"], ph, me, "b", S.snt)
+        left += _send(g, T, topo, rt["second"], ph, me, "p", S.snt)
+        left += _send(g, T, topo, rt["second"], ph, me, "w", S.snt)
     g.wait_ge(S.snt, left)
 
     v = g.vector
-    v.wait_ge(S.lx, 16)
-    v.quantize_mx(T.xq[:, own()], T.xs[:, own()], T.xb[:]).then_inc(S.qx, 1)
-    for i, js, ld, qs in ((0, mine, S.la, S.qa), (1, mine, S.lb, S.qb)):
+    for a in (0, 1):
+        v.wait_ge(S["lx%d" % a], 16)
+        v.quantize_mx(T.xq[:, half(me, a)], T.xs[:, half(me, a)], T.xb[:, half(0, a, 4)]).then_inc(S["qx%d" % a], 1)
+    for i, js, ld, qs in ((0, mine, S.la, S.qa), (1, mine, S.lb, S.qb), (0, far, S.lc, S.qc)):
         v.wait_ge(ld, 16)
         c = w1cols(i, js, WC)
         v.quantize_mx(T.w1q[:, c], T.w1s[:, c], T.w1b[:, w1cols(i, js, 4 * WC)]).then_inc(qs, 1)
-    v.wait_ge(S.l2, 16)
-    v.quantize_mx(T.w2q[:], T.w2s[:], T.w2b[:]).then_inc(S.q2, 1)
-    v.wait_ge(S.lc, 16)
-    c = w1cols(0, far, WC)
-    v.quantize_mx(T.w1q[:, c], T.w1s[:, c], T.w1b[:, w1cols(0, far, 4 * WC)]).then_inc(S.qc, 1)
-    v.wait_ge(S.ld, 16)
-    for n, j in enumerate(far):
-        c = w1cols(1, [j], WC)
-        v.quantize_mx(T.w1q[:, c], T.w1s[:, c], T.w1b[:, w1cols(1, [j], 4 * WC)]).then_inc(S["qd%d" % n], 1)
+    for n, js in enumerate(pairs):
+        v.wait_ge(S["ld%d" % n], 16)
+        for j in sorted(js, key=lambda j: routes[j]["late"]):
+            c = w1cols(1, [j], WC)
+            v.quantize_mx(T.w1q[:, c], T.w1s[:, c], T.w1b[:, w1cols(1, [j], 4 * WC)]).then_inc(S["qd%d" % j], 1)
 
     t = g.tensor
+    seen = set()
 
-    def landed(ph, j):
+    def need(name, val):
+        if name not in seen:
+            seen.add(name)
+            t.wait_ge(S[name], val)
+
+    def landed(ph, j, a):
         if j == me:
-            t.wait_ge(S.qx if ph == "x" else S.qh, 1)
+            need("q%s%d" % (ph, a), 1)
         else:
-            t.wait_ge(S["%sp%d" % (ph, j)], routes[j]["cnt"][core])
-            t.wait_ge(S["%sc%d" % (ph, j)], routes[j]["cnt"][core])
+            n = routes[j]["cnt"][core]
+            need("%sp%d" % (ph, j), n)
+            need("%s%s%d" % (ph, "b" if (a == 1 or core in routes[j]["whole"]) else "a", j), n)
 
-    def mm1(i, j, start, stop):
+    def mm1(i, j, a, ready):
+        need(ready, 1)
+        landed("x", j, a)
         cw = w1cols(i, [j], WC)
-        cx = slice(NC * j, NC * j + NC)
-        return t.matmul_mx(T.ps[:, 512 * i:512 * i + NC], T.w1q[:, cw], T.w1s[:, cw], T.xq[:, cx], T.xs[:, cx],
-                           start, stop)
+        b = 512 * (2 * a + i)
+        ins = t.matmul_mx(T.ps[:, b:b + HC], T.w1q[:, cw], T.w1s[:, cw], T.xq[:, half(j, a)], T.xs[:, half(j, a)],
+                          j == me, j == late[-1])
+        if j == late[-1]:
+            ins.then_inc(S["z%d%d" % (i, a)], 1)
 
-    t.wait_ge(S.qa, 1)
-    for n, j in enumerate([me] + near):
-        landed("x", j)
-        mm1(0, j, n == 0, False)
-        if n == 0:
-            t.wait_ge(S.qb, 1)
-        mm1(1, j, n == 0, False)
-    t.wait_ge(S.qc, 1)
-    early, late = far[:2], far[2:]
-    for j in early:
-        landed("x", j)
-        mm1(0, j, False, False)
-    for n, j in enumerate(early):
-        t.wait_ge(S["qd%d" % n], 1)
-        mm1(1, j, False, False)
-    for n, j in enumerate(late):
-        landed("x", j)
-        ins = mm1(0, j, False, n == 1)
-        if n == 1:
-            ins.then_inc(S.z0, 1)
-    for n, j in enumerate(late):
-        t.wait_ge(S["qd%d" % (2 + n)], 1)
-        ins = mm1(1, j, False, n == 1)
-        if n == 1:
-            ins.then_inc(S.z1, 1)
+    for i, ready in ((0, "qa"), (1, "qb")):
+        for j in [me] + near:
+            for a in (0, 1):
+                mm1(i, j, a, ready)
+    for i in (0, 1):
+        for j in early:
+            for a in (0, 1):
+                mm1(i, j, a, "qc" if i == 0 else "qd%d" % j)
+    for a in (0, 1):
+        for i in (0, 1):
+            for j in late:
+                mm1(i, j, a, "qc" if i == 0 else "qd%d" % j)
 
-    W = 4 * NC
-    v.wait_ge(S.z0, 1)
-    v.tensor_scalar(T.hb[:, 0:W:4], T.ps[:, 0:NC], CACT, 0.0, AluOpType.mult, AluOpType.max).then_inc(S.act, 1)
-    v.tensor_scalar(T.hb[:, 1:W:4], T.ps[:, 0:NC], -CACT, 0.0, AluOpType.mult, AluOpType.max).then_inc(S.act, 1)
-    a = g.scalar
-    a.wait_ge(S.z1, 1)
-    a.activation(T.hb[:, 2:W:4], T.ps[:, 512:512 + NC], ActivationFunctionType.Relu, scale=CACT).then_inc(S.act, 1)
-    a.activation(T.hb[:, 3:W:4], T.ps[:, 512:512 + NC], ActivationFunctionType.Relu, scale=-CACT).then_inc(S.act, 1)
-    v.wait_ge(S.act, 4)
-    v.quantize_mx(T.hq[:, own()], T.hs[:, own()], T.hb[:]).then_inc(S.qh, 1)
+    s = g.scalar
+    for a in (0, 1):
+        lo, hi = 4 * HC * a, 4 * HC * (a + 1)
+        z0 = T.ps[:, 512 * (2 * a):512 * (2 * a) + HC]
+        z1 = T.ps[:, 512 * (2 * a + 1):512 * (2 * a + 1) + HC]
+        act = S["act%d" % a]
+        v.wait_ge(S["z0%d" % a], 1)
+        v.tensor_scalar(T.hb[:, lo + 0:hi:4], z0, CACT, 0.0, AluOpType.mult, AluOpType.max).then_inc(act, 1)
+        v.tensor_scalar(T.hb[:, lo + 1:hi:4], z0, -CACT, 0.0, AluOpType.mult, AluOpType.max).then_inc(act, 1)
+        s.wait_ge(S["z1%d" % a], 1)
+        s.activation(T.hb[:, lo + 2:hi:4], z1, ActivationFunctionType.Relu, scale=CACT).then_inc(act, 1)
+        s.activation(T.hb[:, lo + 3:hi:4], z1, ActivationFunctionType.Relu, scale=-CACT).then_inc(act, 1)
+        v.wait_ge(act, 4)
+        v.quantize_mx(T.hq[:, half(me, a)], T.hs[:, half(me, a)], T.hb[:, lo:hi]).then_inc(S["qh%d" % a], 1)
+    v.wait_ge(S.l2, 16)
+    v.quantize_mx(T.w2q[:], T.w2s[:], T.w2b[:]).then_inc(S.q2, 1)
 
     g.sync.wait_ge(S.gh, gate)
-    g.sync.wait_ge(S.act, 4)
+    g.sync.wait_ge(S.act0, 4)
+    g.sync.wait_ge(S.act1, 4)
     g.sync.dma_start(T.h[:], T.hb[:]).then_inc(S.sts, 16)
-    nsts, nstc = 16, 0
-    t.wait_ge(S.q2, 1)
-    for n, j in enumerate([me] + near + far):
-        b = 512 * ((n + 2) % 8)
-        cy = slice(NC * j, NC * j + NC)
-        landed("h", j)
-        t.matmul_mx(T.ps[:, b:b + NC], T.w2q[:], T.w2s[:], T.hq[:, cy], T.hs[:, cy], True, True).then_inc(
+    done = {"sts": 16, "stc": 0}
+
+    def store(k, cols, sems):
+        qu, name = ((g.sync, "sts"), (s, "stc"))[k % 2]
+        for n in sems:
+            qu.wait_ge(S["c%d" % n], 1)
+        qu.dma_start(T.y[:, cols], T.yb[:, cols]).then_inc(S[name], 16)
+        done[name] += 16
+
+    seq = [(j, a) for j in [me] + near + early for a in (0, 1)] + [(j, a) for a in (0, 1) for j in late]
+    need("q2", 1)
+    for n, (j, a) in enumerate(seq):
+        b = 512 * ((n + 4) % 8)
+        cy = half(j, a)
+        landed("h", j, a)
+        if n >= 8:
+            t.wait_ge(S["c%d" % (n - 8)], 1)
+        t.matmul_mx(T.ps[:, b:b + HC], T.w2q[:], T.w2s[:], T.hq[:, cy], T.hs[:, cy], True, True).then_inc(
             S["y%d" % n], 1)
         if n % 2 == 0:
             v.wait_ge(S["y%d" % n], 1)
-            v.tensor_copy(T.yb[:, cy], T.ps[:, b:b + NC]).then_inc(S["c%d" % n], 1)
-            g.sync.wait_ge(S["c%d" % n], 1)
-            g.sync.dma_start(T.y[:, cy], T.yb[:, cy]).then_inc(S.sts, 16)
-            nsts += 16
+            v.tensor_copy(T.yb[:, cy], T.ps[:, b:b + HC]).then_inc(S["c%d" % n], 1)
         else:
-            a.wait_ge(S["y%d" % n], 1)
-            a.activation(T.yb[:, cy], T.ps[:, b:b + NC], ActivationFunctionType.Copy).then_inc(S["c%d" % n], 1)
-            a.wait_ge(S["c%d" % n], 1)
-            a.dma_start(T.y[:, cy], T.yb[:, cy]).then_inc(S.stc, 16)
-            nstc += 16
-    g.sync.wait_ge(S.sts, nsts)
-    a.wait_ge(S.stc, nstc)
+            s.wait_ge(S["y%d" % n], 1)
+            s.activation(T.yb[:, cy], T.ps[:, b:b + HC], ActivationFunctionType.Copy).then_inc(S["c%d" % n], 1)
+        if j in late:
+            store(n, cy, [n])
+        elif a == 1:
+            store(n // 2, slice(NC * j, NC * j + NC), [n - 1, n])
+    g.sync.wait_ge(S.sts, done["sts"])
+    s.wait_ge(S.stc, done["stc"])

import numpy as np
from concourse.bass import DstId, RemoteDMATransfer
from concourse.mybir import dt, AluOpType, ActivationFunctionType

N = 8
NSIM = 64
NC = 256
HC = NC // 2
WC = 128
CACT = float(np.float32(0.00672))

SCRATCH = {
    "xb": ("sbuf", [128, 4 * NC], "bfloat16"),
    "w1b": ("sbuf", [128, 2 * N * 4 * WC], "bfloat16"),
    "w2b": ("sbuf", [128, 4 * WC], "bfloat16"),
    "hb": ("sbuf", [128, 4 * NC], "bfloat16"),
    "yb": ("sbuf", [128, N * NC], "float32"),
    "xq": ("sbuf", [128, N * NC], "float8_e4m3fn_x4"),
    "xs": ("sbuf", [128, N * NC], "uint8"),
    "hq": ("sbuf", [128, N * NC], "float8_e4m3fn_x4"),
    "hs": ("sbuf", [128, N * NC], "uint8"),
    "w1q": ("sbuf", [128, 2 * N * WC], "float8_e4m3fn_x4"),
    "w1s": ("sbuf", [128, 2 * N * WC], "uint8"),
    "w2q": ("sbuf", [128, WC], "float8_e4m3fn_x4"),
    "w2s": ("sbuf", [128, WC], "uint8"),
    "ps": ("psum", [128, 8 * 512], "float32"),
}
SEMAPHORES = (
    ["%s%s%d" % (ph, k, j) for ph in "xh" for k in "pab" for j in range(N)]
    + ["lx0", "lx1", "la", "lb", "lc", "ld0", "ld1", "l2"]
    + ["qx0", "qx1", "qh0", "qh1", "qa", "qb", "qc", "q2"] + ["qd%d" % j for j in range(N)]
    + ["z%d%d" % (i, a) for i in range(2) for a in range(2)] + ["act0", "act1"]
    + ["y%d" % n for n in range(2 * N)] + ["c%d" % n for n in range(2 * N)]
    + ["gx", "gh", "snt", "sts", "stc"]
)
LONG = ("a", "p", "b")


def _bits(m):
    return bin(m).count("1")


def _plan(T, topo):
    cores = list(T.cores)
    routes = []
    for r in cores:
        near = [c for c in cores if topo.chip(c) == topo.chip(r) and c != r]
        far = [c for c in cores if topo.chip(c) != topo.chip(r)]
        near.sort(key=lambda c: topo.die(c) != topo.die(r))

        def spare(ch, die):
            return [c for c in range(NSIM) if topo.chip(c) == ch and topo.die(c) == die and c not in cores]

        if topo.may_write(r, far[0]):
            carrier = r
        else:
            carrier = [c for c in spare(topo.chip(r), topo.die(r)) if topo.may_write(c, far[0])][0]
        spreader = [c for c in spare(topo.chip(far[0]), topo.die(carrier))
                    if topo.may_write(c, r) == (carrier != r)][0]
        on = topo.mask(r, near[0])
        if carrier == r:
            off = topo.mask(r, spreader)
            rest = on & ~off
            first = [(off, [spreader]), (rest, [near[0]])]
            second = [(off, [near[1]]), (rest, [near[2]])]
            hops = []
        else:
            first = [(on, [carrier])]
            second = [(on, near)]
            hops = [(carrier, [(topo.mask(carrier, spreader), [spreader])])]
        hops.append((spreader, [(topo.mask(spreader, far[0]), far)]))
        cnt = {}
        for parts in [first, second] + [h[1] for h in hops]:
            for m, ds in parts:
                for d in ds:
                    cnt[d] = _bits(m)
        whole = [d for m, ds in second for d in ds]
        routes.append({"first": first, "second": second, "hops": hops, "cnt": cnt, "late": carrier != r,
                       "whole": whole})
    return routes


def _send(g, T, topo, parts, ph, j, kind, local_sem):
    q, s = (T.xq, T.xs) if ph == "x" else (T.hq, T.hs)
    lo = NC * j + (HC if kind == "b" else 0)
    hi = NC * j + (HC if kind == "a" else NC)
    remote_sem = T.sem["%s%s%d" % (ph, "b" if kind == "w" else kind, j)]

    def view():
        return s[:, lo:hi] if kind == "p" else q[:, lo:hi].bitcast(dt.uint8)

    if len(parts) == 1 and len(parts[0][1]) == 1:
        m, ds = parts[0]
        rid, pid, _se = topo.addr(ds[0])
        g.remote_dma(out_ap=view(), in_ap=view(), remote_sem=remote_sem, local_sem=local_sem, pid=pid,
                     routing_id=rid, dma_engine_mask=m)
        return _bits(m)
    trs = []
    for m, ds in parts:
        ids = [DstId(rid=topo.addr(d)[0], pnc=topo.addr(d)[1]) for d in ds]
        trs.append(RemoteDMATransfer(dst_ids=ids, dma_engine_mask=m, remote_sem=remote_sem,
                                     srcs=[view()], dsts=[view() for d in ds]))
    g.remote_dma_fused(trs, local_sem=local_sem)
    return sum(_bits(m) for m, ds in parts)


def _spare_program(g, core, T, topo, routes):
    jobs = []
    for depth in (0, 1):
        for j, rt in enumerate(routes):
            hops = rt["hops"]
            for n, (who, parts) in enumerate(hops):
                if who == core and (n == len(hops) - 1) == (depth == 1):
                    jobs.append((j, parts, rt["cnt"][core]))
    if not jobs:
        return
    left = 0
    for ph in "xh":
        for j, parts, cnt in jobs:
            for kind in LONG:
                g.wait_ge(T.sem["%s%s%d" % (ph, kind, j)], cnt)
                left += _send(g, T, topo, parts, ph, j, kind, T.sem.snt)
    g.wait_ge(T.sem.snt, left)


def rank_program(g, core, T, topo):
    routes = _plan(T, topo)
    me = T.rank_of(core)
    if me is None:
        _spare_program(g, core, T, topo, routes)
        return
    S = T.sem
    cores = list(T.cores)
    mine = [j for j in range(N) if topo.chip(cores[j]) == topo.chip(core)]
    far = [j for j in range(N) if j not in mine]
    near = sorted([j for j in mine if j != me], key=lambda j: (topo.die(cores[j]) != topo.die(core), routes[j]["late"]))
    pairs = [sorted(far)[:2], sorted(far)[2:]]
    early = [j for j in sorted(far) if not routes[j]["late"]]
    late = [j for j in sorted(far) if routes[j]["late"]]
    rt = routes[me]

    def w1cols(i, js, w):
        return slice(w * (N * i + min(js)), w * (N * i + max(js) + 1))

    def half(j, a, w=1):
        return slice(w * (NC * j + HC * a), w * (NC * j + HC * a + HC))

    gate = sum(_bits(m) for m, ds in rt["first"])
    g.sync.dma_start(T.xb[:, half(0, 0, 4)], T.x[:, half(0, 0, 4)]).then_inc(S.lx0, 16)
    g.scalar.dma_start(T.xb[:, half(0, 1, 4)], T.x[:, half(0, 1, 4)]).then_inc(S.lx1, 16)
    c = w1cols(0, mine, 4 * WC)
    g.sync.dma_start(T.w1b[:, c], T.w1[:, c]).then_inc(S.la, 16)
    g.sync.wait_ge(S.gx, gate)
    for i, js, ld in ((1, mine, S.lb), (0, far, S.lc), (1, pairs[0], S.ld0), (1, pairs[1], S.ld1)):
        c = w1cols(i, js, 4 * WC)
        g.sync.dma_start(T.w1b[:, c], T.w1[:, c]).then_inc(ld, 16)
    g.sync.dma_start(T.w2b[:], T.w2[:]).then_inc(S.l2, 16)

    left = 0
    for ph, gsem in (("x", S.gx), ("h", S.gh)):
        g.wait_ge(S["q%s0" % ph], 1)
        _send(g, T, topo, rt["first"], ph, me, "a", gsem)
        g.wait_ge(S["q%s1" % ph], 1)
        left += _send(g, T, topo, rt["first"], ph, me, "p", S.snt)
        left += _send(g, T, topo, rt["first"], ph, me, "b", S.snt)
        left += _send(g, T, topo, rt["second"], ph, me, "p", S.snt)
        left += _send(g, T, topo, rt["second"], ph, me, "w", S.snt)
    g.wait_ge(S.snt, left)

    v = g.vector
    for a in (0, 1):
        v.wait_ge(S["lx%d" % a], 16)
        v.quantize_mx(T.xq[:, half(me, a)], T.xs[:, half(me, a)], T.xb[:, half(0, a, 4)]).then_inc(S["qx%d" % a], 1)
    for i, js, ld, qs in ((0, mine, S.la, S.qa), (1, mine, S.lb, S.qb), (0, far, S.lc, S.qc)):
        v.wait_ge(ld, 16)
        c = w1cols(i, js, WC)
        v.quantize_mx(T.w1q[:, c], T.w1s[:, c], T.w1b[:, w1cols(i, js, 4 * WC)]).then_inc(qs, 1)
    for n, js in enumerate(pairs):
        v.wait_ge(S["ld%d" % n], 16)
        for j in sorted(js, key=lambda j: routes[j]["late"]):
            c = w1cols(1, [j], WC)
            v.quantize_mx(T.w1q[:, c], T.w1s[:, c], T.w1b[:, w1cols(1, [j], 4 * WC)]).then_inc(S["qd%d" % j], 1)

    t = g.tensor
    seen = set()

    def need(name, val):
        if name not in seen:
            seen.add(name)
            t.wait_ge(S[name], val)

    def landed(ph, j, a):
        if j == me:
            need("q%s%d" % (ph, a), 1)
        else:
            n = routes[j]["cnt"][core]
            need("%sp%d" % (ph, j), n)
            need("%s%s%d" % (ph, "b" if (a == 1 or core in routes[j]["whole"]) else "a", j), n)

    def mm1(i, j, a, ready):
        need(ready, 1)
        landed("x", j, a)
        cw = w1cols(i, [j], WC)
        b = 512 * (2 * a + i)
        ins = t.matmul_mx(T.ps[:, b:b + HC], T.w1q[:, cw], T.w1s[:, cw], T.xq[:, half(j, a)], T.xs[:, half(j, a)],
                          j == me, j == late[-1])
        if j == late[-1]:
            ins.then_inc(S["z%d%d" % (i, a)], 1)

    for i, ready in ((0, "qa"), (1, "qb")):
        for j in [me] + near:
            for a in (0, 1):
                mm1(i, j, a, ready)
    for i in (0, 1):
        for j in early:
            for a in (0, 1):
                mm1(i, j, a, "qc" if i == 0 else "qd%d" % j)
    for a in (0, 1):
        for i in (0, 1):
            for j in late:
                mm1(i, j, a, "qc" if i == 0 else "qd%d" % j)

    s = g.scalar
    for a in (0, 1):
        lo, hi = 4 * HC * a, 4 * HC * (a + 1)
        z0 = T.ps[:, 512 * (2 * a):512 * (2 * a) + HC]
        z1 = T.ps[:, 512 * (2 * a + 1):512 * (2 * a + 1) + HC]
        act = S["act%d" % a]
        v.wait_ge(S["z0%d" % a], 1)
        v.tensor_scalar(T.hb[:, lo + 0:hi:4], z0, CACT, 0.0, AluOpType.mult, AluOpType.max).then_inc(act, 1)
        v.tensor_scalar(T.hb[:, lo + 1:hi:4], z0, -CACT, 0.0, AluOpType.mult, AluOpType.max).then_inc(act, 1)
        s.wait_ge(S["z1%d" % a], 1)
        s.activation(T.hb[:, lo + 2:hi:4], z1, ActivationFunctionType.Relu, scale=CACT).then_inc(act, 1)
        s.activation(T.hb[:, lo + 3:hi:4], z1, ActivationFunctionType.Relu, scale=-CACT).then_inc(act, 1)
        v.wait_ge(act, 4)
        v.quantize_mx(T.hq[:, half(me, a)], T.hs[:, half(me, a)], T.hb[:, lo:hi]).then_inc(S["qh%d" % a], 1)
    v.wait_ge(S.l2, 16)
    v.quantize_mx(T.w2q[:], T.w2s[:], T.w2b[:]).then_inc(S.q2, 1)

    g.sync.wait_ge(S.gh, gate)
    g.sync.wait_ge(S.act0, 4)
    g.sync.wait_ge(S.act1, 4)
    g.sync.dma_start(T.h[:], T.hb[:]).then_inc(S.sts, 16)
    done = {"sts": 16, "stc": 0}

    def store(k, cols, sems):
        qu, name = ((g.sync, "sts"), (s, "stc"))[k % 2]
        for n in sems:
            qu.wait_ge(S["c%d" % n], 1)
        qu.dma_start(T.y[:, cols], T.yb[:, cols]).then_inc(S[name], 16)
        done[name] += 16

    seq = [(j, a) for j in [me] + near + early for a in (0, 1)] + [(j, a) for a in (0, 1) for j in late]
    need("q2", 1)
    for n, (j, a) in enumerate(seq):
        b = 512 * ((n + 4) % 8)
        cy = half(j, a)
        landed("h", j, a)
        if n >= 8:
            t.wait_ge(S["c%d" % (n - 8)], 1)
        t.matmul_mx(T.ps[:, b:b + HC], T.w2q[:], T.w2s[:], T.hq[:, cy], T.hs[:, cy], True, True).then_inc(
            S["y%d" % n], 1)
        if n % 2 == 0:
            v.wait_ge(S["y%d" % n], 1)
            v.tensor_copy(T.yb[:, cy], T.ps[:, b:b + HC]).then_inc(S["c%d" % n], 1)
        else:
            s.wait_ge(S["y%d" % n], 1)
            s.activation(T.yb[:, cy], T.ps[:, b:b + HC], ActivationFunctionType.Copy).then_inc(S["c%d" % n], 1)
        if j in late:
            store(n, cy, [n])
        elif a == 1:
            store(n // 2, slice(NC * j, NC * j + NC), [n - 1, n])
    g.sync.wait_ge(S.sts, done["sts"])
    s.wait_ge(S.stc, done["stc"])
